import numpy as np
import ml_dtypes


def mxq(x, axis, fmt="e4m3"):
    dtype, down = {"e4m3": (ml_dtypes.float8_e4m3fn, 7), "e5m2": (ml_dtypes.float8_e5m2, 14)}[fmt]
    v = np.moveaxis(np.asarray(x, np.float32).astype(ml_dtypes.bfloat16).astype(np.float64), axis, -1)
    blocks = v.reshape(v.shape[:-1] + (-1, 32))
    amax = np.abs(blocks).max(-1, keepdims=True)
    byte = np.maximum(np.where(amax > 0, np.frexp(amax)[1] - 1 + 127, 0) - down, 1)
    scale = np.exp2(byte - 127.0)
    codes = (blocks / scale).astype(np.float32).astype(dtype).astype(np.float64)
    return np.moveaxis((codes * scale).reshape(v.shape), -1, axis)


WIDE = False


def mx_kscale(k):
    if not WIDE:
        return np.ones(k)
    levels = np.array([30, -30])
    if k % 512:
        return np.exp2(np.random.permutation(np.resize(levels, k // 32))).repeat(32)
    a = np.empty((k // 512, 16))
    for p in range(k // 512):
        a[p, :8] = np.random.permutation(np.resize(levels, 8))
        for g in range(8):
            far = levels[np.abs(levels - a[p, g]) >= 10]
            a[p, g + 8] = far[np.random.randint(len(far))]
    return np.exp2(a.ravel()).repeat(32)


def f64(x):
    return np.asarray(x).astype(np.float64)


def striped(idx):
    return np.tile(idx.reshape(-1, 16).T, (8, 1)).astype(np.uint16)


def unstriped(offs):
    return offs[:16].T.reshape(-1).astype(np.int64)


E2M1 = np.array([0.0, 0.5, 1.0, 1.5, 2.0, 3.0, 4.0, 6.0, -0.0, -0.5, -1.0, -1.5, -2.0, -3.0, -4.0, -6.0])


def pack_weight(w, fmt):
    k, n = w.shape
    w = f64(np.asarray(w, np.float32).astype(ml_dtypes.bfloat16)).reshape(k // 32, 32, n)
    amax = np.abs(w).max(1)
    if fmt == "e4m3":
        byte = np.frexp(amax)[1] - 1 + 127 - 7
    elif fmt == "e5m2":
        byte = np.frexp(amax)[1] - 1 + 127 - 14
    else:
        mant, ex = np.frexp(amax / 6.0)
        byte = np.where(mant > 0.5, ex, ex - 1) + 127
    byte = np.clip(np.where(amax > 0, byte, 1), 1, 254)
    scaled = (w * np.exp2(127.0 - byte)[:, None, :]).reshape(k, n).astype(np.float32)
    by_word = np.ascontiguousarray(scaled.reshape(k // 512, 128, 4, n).transpose(0, 1, 3, 2))
    if fmt == "e4m3":
        words = by_word.astype(ml_dtypes.float8_e4m3fn).view(np.uint8)
    elif fmt == "e5m2":
        words = by_word.astype(ml_dtypes.float8_e5m2).view(np.uint8)
    else:
        c = by_word.astype(ml_dtypes.float4_e2m1fn).view(np.uint8) & 0xF
        words = (c[..., 0::2] | (c[..., 1::2] << 4)).reshape(k // 512, 128, 2 * n)
    return np.ascontiguousarray(words), np.ascontiguousarray(byte.astype(np.uint8).reshape(k // 512, 16, n))


def unpack_weight(words, scales, fmt):
    g, _, n = scales.shape
    words = np.ascontiguousarray(words).reshape(g, 128, n, -1)
    if fmt == "e4m3":
        vals = words.view(ml_dtypes.float8_e4m3fn).astype(np.float64)
    elif fmt == "e5m2":
        vals = words.view(ml_dtypes.float8_e5m2).astype(np.float64)
    else:
        nib = np.empty((g, 128, n, 4), np.uint8)
        nib[..., 0::2] = words & 0xF
        nib[..., 1::2] = words >> 4
        vals = E2M1[nib]
    vals = vals * np.repeat(np.exp2(scales.astype(np.float64) - 127.0), 8, axis=1)[..., None]
    return vals.transpose(0, 1, 3, 2).reshape(g * 512, n)


K, T, E, C, N = 384, 1280, 5, 512, 1024


def by_expert(wq, xq):
    return np.concatenate([wq[e].T @ xq[:, e * C:(e + 1) * C] for e in range(E)], axis=1)


def setup_inputs():
    n = np.random.standard_normal
    s = mx_kscale(N)[:, None]
    first = np.random.permutation(np.repeat(np.arange(E), T // E))
    second = (first + 1 + np.random.permutation(np.repeat(np.arange(E - 1), -(-T // (E - 1)))[:T])) % E
    while np.bincount(second, minlength=E).max() != T // E:
        load = np.bincount(second, minlength=E); hi, lo = int(load.argmax()), int(load.argmin())
        t = np.flatnonzero((second == hi) & (first != lo))[0]; second[t] = lo
    slot_token = np.empty(E * C, np.int64); pos = np.empty((2, T), np.int64); fill = np.zeros(E, np.int64)
    place = np.stack([np.random.permutation(C) for _ in range(E)])
    for r, deal in enumerate((first, second)):
        for t in np.random.permutation(T):
            e = deal[t]; j = e * C + place[e, fill[e]]; fill[e] += 1; slot_token[j] = t; pos[r, t] = j
    g = np.random.uniform(0.2, 0.8, T)
    w_slot = np.empty(E * C); w_slot[pos[0]] = g; w_slot[pos[1]] = 1.0 - g
    dy = pack_weight(n((N, T)) * s, "e5m2")
    return {
        "dy_words": dy[0],
        "dy_scales": dy[1],
        "w": (n((E, N, K)) / np.sqrt(N) / s[None]).astype(np.float32),
        "gate": np.tile(w_slot, (K, 1)).astype(np.float32),
        "offs": striped(slot_token),
        "pos1": striped(pos[0]),
        "pos2": striped(pos[1]),
    }


def reference(dy_words, dy_scales, w, gate, offs, pos1, pos2):
    idx = unstriped(offs)
    gq = unpack_weight(dy_words, dy_scales, "e5m2")[:, idx]
    dx = f64(gate) * by_expert(mxq(f64(w), 1, "e4m3"), gq)
    return dx[:, unstriped(pos1)] + dx[:, unstriped(pos2)]

@@ -1,0 +1,185 @@
+from contextlib import ExitStack
+
+import concourse.mybir as mybir
+
+K, T, E, C, N = 384, 1280, 5, 512, 1024
+S = E * C
+FLOPS = 2 * N * K * S
+BYTES = N * T + N // 32 * T + 4 * E * N * K + 4 * S + 2 * 128 * (S + 2 * T) // 16 + 4 * K * T
+
+F32 = mybir.dt.float32
+BF16 = mybir.dt.bfloat16
+I32 = mybir.dt.int32
+U32 = mybir.dt.uint32
+U16 = mybir.dt.uint16
+U8 = mybir.dt.uint8
+E4X4 = mybir.dt.float8_e4m3fn_x4
+E5X4 = mybir.dt.float8_e5m2_x4
+MULT = mybir.AluOpType.mult
+ADD = mybir.AluOpType.add
+
+P = 128
+PASSES = 2
+ALIGN = 64
+EARLY = 256
+LATE = K - EARLY
+SCALE_WINDOW = 2048
+SCALE_CUT = 2 * C
+
+
+def tile_moe_bdx_lin_none_kernel(tc, dy_words, dy_scales, w, gate, offs, pos1, pos2, out):
+    nc = tc.nc
+    with ExitStack() as ctx:
+        keep = ctx.enter_context(tc.tile_pool(name="keep", bufs=1))
+        psum = ctx.enter_context(tc.psum_pool(name="psum", bufs=8))
+
+        def sb(shape, dtype, name, tag=None):
+            return keep.tile(shape, dtype, name=name, tag=tag or name, align_bytes=ALIGN)
+
+        offs_t = keep.tile([P, S // 16], U16, name="offs_t")
+        pos1_t = keep.tile([P, T // 16], U16, name="pos1_t")
+        pos2_t = keep.tile([P, T // 16], U16, name="pos2_t")
+        nc.sync.dma_start(offs_t[:], offs)
+
+        scale_win = sb([P, SCALE_WINDOW], U8, "scale_win")
+        nc.vector.memset(scale_win[:].bitcast(I32), 0)
+        for q in range(4):
+            nc.scalar.dma_start(
+                scale_win[32 * q : 32 * q + 8, 0:T].bitcast(I32),
+                dy_scales[:, 4 * q : 4 * q + 4, :].bitcast(I32),
+            )
+        word_win = []
+        for o in range(PASSES):
+            t = sb([P, T], U32, "word_win%d" % o)
+            nc.sync.dma_start(t[:].bitcast(I32), dy_words[o].rearrange("p t d -> p (t d)").bitcast(I32))
+            word_win.append(t)
+
+        cuts = ((0, SCALE_CUT), (SCALE_CUT, S))
+        planes = []
+        for i, (a, b) in enumerate(cuts):
+            both = sb([P, b - a], U8, "plane_both%d" % i)
+            second = sb([P, b - a], U8, "plane_second%d" % i)
+            nc.gpsimd.memset(second[:].bitcast(I32), 0)
+            nc.vector.tensor_copy(both[:], scale_win[:].indirect(offs_t[:, a // 16 : b // 16]))
+            planes.append((both, second))
+
+        def shift(i, queue):
+            both, second = planes[i]
+            queue.dma_start(second[0:112, :].bitcast(I32), both[4:116, :].bitcast(I32))
+
+        shift(0, nc.scalar)
+
+        def dy_scale(e, o):
+            i = 0 if e * C < SCALE_CUT else 1
+            a = e * C - cuts[i][0]
+            return planes[i][o][:, a : a + C]
+
+        words = {}
+
+        def gather_words(e, tag):
+            t = sb([P, PASSES * C], U32, "words%d" % e, tag)
+            for o in range(PASSES):
+                nc.vector.tensor_copy(
+                    t[:, o * C : (o + 1) * C],
+                    word_win[o][:].indirect(offs_t[:, e * C // 16 : (e + 1) * C // 16]),
+                )
+            words[e] = t
+
+        gather_words(0, None)
+
+        gate_t = sb([P, S], F32, "gate_t")
+        raw = {}
+
+        def load_w(e, k0, k1, part):
+            for o in range(PASSES):
+                t = sb([P, 4, k1 - k0], F32, "raw_%s_%d_%d" % (part, e, o))
+                nc.sync.dma_start(
+                    t[:], w[e, o * 512 : (o + 1) * 512, k0:k1].rearrange("(p j) k -> p j k", j=4)
+                )
+                raw[(part, e, o)] = t
+
+        for e in range(E):
+            load_w(e, 0, EARLY, "early")
+            if e == 1:
+                shift(1, nc.sync)
+            if e >= 1:
+                nc.sync.dma_start(gate_t[:, (e - 1) * C : e * C], gate[0:P, (e - 1) * C : e * C])
+        nc.sync.dma_start(gate_t[:, (E - 1) * C : S], gate[0:P, (E - 1) * C : S])
+        nc.sync.dma_start(pos1_t[:], pos1)
+        nc.sync.dma_start(pos2_t[:], pos2)
+        for e in range(E):
+            load_w(e, EARLY, K, "late")
+
+        codes = {}
+
+        def quantize(part, experts, width):
+            name = "%s_%d" % (part, experts[0])
+            cols = len(experts) * PASSES * width
+            grouped = sb([P, cols * 4], BF16, "grouped_" + name)
+            cw = sb([P, cols], U32, "codes_" + name)
+            cs = sb([P, cols], U8, "scales_" + name)
+            for n, e in enumerate(experts):
+                for o in range(PASSES):
+                    c0 = (n * PASSES + o) * width
+                    nc.scalar.copy(
+                        grouped[:, 4 * c0 : 4 * (c0 + width)].rearrange("p (c i t) -> p c t i", i=4, t=4),
+                        raw[(part, e, o)][:].rearrange("p t (c i) -> p c t i", i=4),
+                    )
+                    codes[(part, e, o)] = (cw[:, c0 : c0 + width], cs[:, c0 : c0 + width])
+            nc.vector.quantize_mx(out=cw[:].bitcast(E4X4), scales=cs[:], in_=grouped[:])
+
+        dx = [sb([P, S], F32, "dx%d" % b) for b in range(K // P)]
+
+        def multiply(e, b):
+            part, c0 = ("early", b * P) if b * P < EARLY else ("late", b * P - EARLY)
+            acc = psum.tile([P, C], F32, name="acc")
+            for o in range(PASSES):
+                cw, cs = codes[(part, e, o)]
+                nc.tensor.matmul_mx(
+                    out=acc[:],
+                    lhsT=cw[:, c0 : c0 + P].bitcast(E4X4),
+                    lhsT_scale=cs[:, c0 : c0 + P],
+                    rhs=words[e][:, o * C : (o + 1) * C].bitcast(E5X4),
+                    rhs_scale=dy_scale(e, o),
+                    start=(o == 0),
+                    stop=(o == PASSES - 1),
+                )
+            cols = slice(e * C, (e + 1) * C)
+            nc.vector.tensor_tensor(dx[b][:, cols], acc[:], gate_t[:, cols], MULT)
+
+        def fetch_first(b, pieces, tag):
+            first = sb([P, T], F32, "first%d" % b, tag)
+            for a, z in pieces:
+                nc.vector.tensor_copy(first[:, a:z], dx[b][:].indirect(pos1_t[:, a // 16 : z // 16]))
+            return first
+
+        def fetch_second(b, first, pieces):
+            total = sb([P, T], F32, "total%d" % b)
+            for a, z in pieces:
+                nc.vector.tensor_tensor(
+                    total[:, a:z], dx[b][:].indirect(pos2_t[:, a // 16 : z // 16]), first[:, a:z], ADD
+                )
+                nc.sync.dma_start(out[b * P : (b + 1) * P, a:z], total[:, a:z])
+
+        for e in range(3):
+            quantize("early", [e], EARLY)
+            gather_words(e + 1, "raw_early_%d_1" % e)
+            for b in range(2):
+                multiply(e, b)
+        quantize("early", [3, 4], EARLY)
+        gather_words(4, "raw_early_4_1")
+        for e in (3, 4):
+            for b in range(2):
+                multiply(e, b)
+
+        halves = ((0, 640), (640, T))
+        first0 = fetch_first(0, halves, None)
+        fetch_second(0, first0, halves)
+        quantize("late", [0, 1, 2, 3], LATE)
+        quantize("late", [4], LATE)
+        first1 = fetch_first(1, halves, "raw_late_4_1")
+        fetch_second(1, first1, halves)
+        for e in range(E):
+            multiply(e, 2)
+        first2 = fetch_first(2, halves, None)
+        fetch_second(2, first2, ((0, 640), (640, 960), (960, T)))

@@ -21,20 +21,44 @@ ADD = mybir.AluOpType.add
 P = 128
 PASSES = 2
 ALIGN = 64
-EARLY = 256
-LATE = K - EARLY
 SCALE_WINDOW = 2048
 SCALE_CUT = 2 * C
+KB = 1024
 
 
 def tile_moe_bdx_lin_none_kernel(tc, dy_words, dy_scales, w, gate, offs, pos1, pos2, out):
     nc = tc.nc
     with ExitStack() as ctx:
         keep = ctx.enter_context(tc.tile_pool(name="keep", bufs=1))
-        psum = ctx.enter_context(tc.psum_pool(name="psum", bufs=8))
+        arena = ctx.enter_context(tc.tile_pool(name="arena", bufs=1))
+        psum = ctx.enter_context(tc.psum_pool(name="psum", bufs=1))
 
-        def sb(shape, dtype, name, tag=None):
-            return keep.tile(shape, dtype, name=name, tag=tag or name, align_bytes=ALIGN)
+        at = {}
+        at["word_win0"] = at["first2"] = 0
+        at["word_win1"] = at["total2"] = 5 * KB
+        at["raw_0_0_1"] = at["words1"] = 10 * KB
+        at["raw_1_0_1"] = at["sumsA"] = 16 * KB
+        at["words2"] = 21 * KB
+        at["sumsB"] = 25 * KB
+        at["raw_3_0_1"] = 26 * KB
+        at["words3"] = 27 * KB
+        at["sumsC"] = 31 * KB
+        at["raw_4_0_1"] = 34 * KB
+        at["words4"] = 35 * KB
+        at["raw_2_128_1"] = at["sumsD"] = 39 * KB
+        at["raw_3_128_1"] = at["first0"] = 41 * KB
+        at["sumsE"] = at["total0"] = 46 * KB
+        at["raw_4_128_1"] = 53 * KB
+        at["second0"] = 54 * KB
+        at["raw_3_256_1"] = at["first1"] = 59 * KB
+        at["sumsF"] = at["total1"] = 64 * KB
+        at["raw_4_256_1"] = 67 * KB + 512
+        at["second1"] = 69 * KB
+
+        def sb(shape, dtype, name):
+            if name in at:
+                return arena.tile(shape, dtype, name=name, align_bytes=ALIGN, offset=at[name])
+            return keep.tile(shape, dtype, name=name, align_bytes=ALIGN)
 
         offs_t = keep.tile([P, S // 16], U16, name="offs_t")
         pos1_t = keep.tile([P, T // 16], U16, name="pos1_t")
@@ -42,32 +66,44 @@ def tile_moe_bdx_lin_none_kernel(tc, dy_words, dy_scales, w, gate, offs, pos1, p
         nc.sync.dma_start(offs_t[:], offs)
 
         scale_win = sb([P, SCALE_WINDOW], U8, "scale_win")
-        nc.vector.memset(scale_win[:].bitcast(I32), 0)
+        nc.gpsimd.memset(scale_win[:].bitcast(I32), 0)
         for q in range(4):
             nc.scalar.dma_start(
                 scale_win[32 * q : 32 * q + 8, 0:T].bitcast(I32),
                 dy_scales[:, 4 * q : 4 * q + 4, :].bitcast(I32),
             )
+        warm = sb([P, 16], F32, "warm")
+        nc.gpsimd.memset(warm[:], 0.0)
+        nc.scalar.copy(warm[:, 8:9], warm[:, 0:1])
+
+        raw = {}
+
+        def load_w(e, k0, k1, passes=(0, 1)):
+            for o in passes:
+                t = sb([P, 4, k1 - k0], F32, "raw_%d_%d_%d" % (e, k0, o))
+                nc.sync.dma_start(
+                    t[:], w[e, o * 512 : (o + 1) * 512, k0:k1].rearrange("(p j) k -> p j k", j=4)
+                )
+                raw[(e, k0, o)] = t
+
         word_win = []
         for o in range(PASSES):
             t = sb([P, T], U32, "word_win%d" % o)
             nc.sync.dma_start(t[:].bitcast(I32), dy_words[o].rearrange("p t d -> p (t d)").bitcast(I32))
             word_win.append(t)
+            load_w(0, 0, K, (o,))
 
         cuts = ((0, SCALE_CUT), (SCALE_CUT, S))
-        planes = []
-        for i, (a, b) in enumerate(cuts):
+        planes = {}
+
+        def gather_scales(i, queue):
+            a, b = cuts[i]
             both = sb([P, b - a], U8, "plane_both%d" % i)
             second = sb([P, b - a], U8, "plane_second%d" % i)
             nc.gpsimd.memset(second[:].bitcast(I32), 0)
             nc.vector.tensor_copy(both[:], scale_win[:].indirect(offs_t[:, a // 16 : b // 16]))
-            planes.append((both, second))
-
-        def shift(i, queue):
-            both, second = planes[i]
             queue.dma_start(second[0:112, :].bitcast(I32), both[4:116, :].bitcast(I32))
-
-        shift(0, nc.scalar)
+            planes[i] = (both, second)
 
         def dy_scale(e, o):
             i = 0 if e * C < SCALE_CUT else 1
@@ -76,44 +112,39 @@ def tile_moe_bdx_lin_none_kernel(tc, dy_words, dy_scales, w, gate, offs, pos1, p
 
         words = {}
 
-        def gather_words(e, tag):
-            t = sb([P, PASSES * C], U32, "words%d" % e, tag)
-            for o in range(PASSES):
-                nc.vector.tensor_copy(
-                    t[:, o * C : (o + 1) * C],
-                    word_win[o][:].indirect(offs_t[:, e * C // 16 : (e + 1) * C // 16]),
-                )
-            words[e] = t
+        word_tiles = {}
 
-        gather_words(0, None)
+        def gather_words(e, passes=(0, 1)):
+            if e not in word_tiles:
+                word_tiles[e] = sb([P, PASSES * C], U32, "words%d" % e)
+            for o in passes:
+                words[(e, o)] = word_tiles[e][:, o * C : (o + 1) * C]
+                nc.vector.tensor_copy(
+                    words[(e, o)], word_win[o][:].indirect(offs_t[:, e * C // 16 : (e + 1) * C // 16])
+                )
+
+        gather_scales(0, nc.scalar)
+        gather_words(0, (0,))
+        gather_scales(1, nc.gpsimd)
+        gather_words(0, (1,))
 
         gate_t = sb([P, S], F32, "gate_t")
-        raw = {}
-
-        def load_w(e, k0, k1, part):
-            for o in range(PASSES):
-                t = sb([P, 4, k1 - k0], F32, "raw_%s_%d_%d" % (part, e, o))
-                nc.sync.dma_start(
-                    t[:], w[e, o * 512 : (o + 1) * 512, k0:k1].rearrange("(p j) k -> p j k", j=4)
-                )
-                raw[(part, e, o)] = t
-
-        for e in range(E):
-            load_w(e, 0, EARLY, "early")
-            if e == 1:
-                shift(1, nc.sync)
-            if e >= 1:
-                nc.sync.dma_start(gate_t[:, (e - 1) * C : e * C], gate[0:P, (e - 1) * C : e * C])
-        nc.sync.dma_start(gate_t[:, (E - 1) * C : S], gate[0:P, (E - 1) * C : S])
+        load_w(1, 0, K)
+        nc.sync.dma_start(gate_t[:, 0 : 2 * C], gate[0:P, 0 : 2 * C])
+        for e in (2, 3, 4):
+            load_w(e, 0, P)
+        nc.sync.dma_start(gate_t[:, 2 * C : S], gate[0:P, 2 * C : S])
         nc.sync.dma_start(pos1_t[:], pos1)
         nc.sync.dma_start(pos2_t[:], pos2)
-        for e in range(E):
-            load_w(e, EARLY, K, "late")
+        for b in (1, 2):
+            for e in (2, 3, 4):
+                load_w(e, b * P, (b + 1) * P)
 
         codes = {}
 
-        def quantize(part, experts, width):
-            name = "%s_%d" % (part, experts[0])
+        def quantize(experts, k0, k1, between=None):
+            name = "%d_%d" % (experts[0], k0)
+            width = k1 - k0
             cols = len(experts) * PASSES * width
             grouped = sb([P, cols * 4], BF16, "grouped_" + name)
             cw = sb([P, cols], U32, "codes_" + name)
@@ -123,63 +154,99 @@ def tile_moe_bdx_lin_none_kernel(tc, dy_words, dy_scales, w, gate, offs, pos1, p
                     c0 = (n * PASSES + o) * width
                     nc.scalar.copy(
                         grouped[:, 4 * c0 : 4 * (c0 + width)].rearrange("p (c i t) -> p c t i", i=4, t=4),
-                        raw[(part, e, o)][:].rearrange("p t (c i) -> p c t i", i=4),
+                        raw[(e, k0, o)][:].rearrange("p t (c i) -> p c t i", i=4),
                     )
-                    codes[(part, e, o)] = (cw[:, c0 : c0 + width], cs[:, c0 : c0 + width])
-            nc.vector.quantize_mx(out=cw[:].bitcast(E4X4), scales=cs[:], in_=grouped[:])
+                    for k in range(k0, k1, P):
+                        c = c0 + k - k0
+                        codes[(e, k // P, o)] = (cw[:, c : c + P], cs[:, c : c + P])
+                if between and n == 0:
+                    between()
+            for a, z in ((0, 512), (512, 768)) if cols == 768 else ((0, cols),):
+                nc.vector.quantize_mx(out=cw[:, a:z].bitcast(E4X4), scales=cs[:, a:z], in_=grouped[:, 4 * a : 4 * z])
 
         dx = [sb([P, S], F32, "dx%d" % b) for b in range(K // P)]
+        acc = {}
 
-        def multiply(e, b):
-            part, c0 = ("early", b * P) if b * P < EARLY else ("late", b * P - EARLY)
-            acc = psum.tile([P, C], F32, name="acc")
+        def multiply(e, b, bank):
+            acc[(e, b)] = psum.tile([P, C], F32, name="acc%d_%d" % (e, b), tag="bank%d" % bank)
             for o in range(PASSES):
-                cw, cs = codes[(part, e, o)]
+                cw, cs = codes[(e, b, o)]
                 nc.tensor.matmul_mx(
-                    out=acc[:],
-                    lhsT=cw[:, c0 : c0 + P].bitcast(E4X4),
-                    lhsT_scale=cs[:, c0 : c0 + P],
-                    rhs=words[e][:, o * C : (o + 1) * C].bitcast(E5X4),
+                    out=acc[(e, b)][:],
+                    lhsT=cw.bitcast(E4X4),
+                    lhsT_scale=cs,
+                    rhs=words[(e, o)].bitcast(E5X4),
                     rhs_scale=dy_scale(e, o),
                     start=(o == 0),
                     stop=(o == PASSES - 1),
                 )
+
+        def gate_direct(e, b):
             cols = slice(e * C, (e + 1) * C)
-            nc.vector.tensor_tensor(dx[b][:, cols], acc[:], gate_t[:, cols], MULT)
+            nc.vector.tensor_tensor(dx[b][:, cols], acc[(e, b)][:], gate_t[:, cols], MULT)
 
-        def fetch_first(b, pieces, tag):
-            first = sb([P, T], F32, "first%d" % b, tag)
-            for a, z in pieces:
-                nc.vector.tensor_copy(first[:, a:z], dx[b][:].indirect(pos1_t[:, a // 16 : z // 16]))
-            return first
+        def gate_staged(name, units):
+            sums = sb([P, len(units) * C], F32, name)
+            for n, (e, b) in enumerate(units):
+                cols = slice(e * C, (e + 1) * C)
+                nc.scalar.copy(sums[:, n * C : (n + 1) * C], acc[(e, b)][:])
+                nc.gpsimd.tensor_tensor(dx[b][:, cols], sums[:, n * C : (n + 1) * C], gate_t[:, cols], MULT)
 
-        def fetch_second(b, first, pieces):
+        def fetch(b, pos_t, name):
+            t = sb([P, T], F32, name)
+            nc.vector.tensor_copy(t[:], dx[b][:].indirect(pos_t[:]))
+            return t
+
+        def add_and_store(b, first, second):
             total = sb([P, T], F32, "total%d" % b)
-            for a, z in pieces:
-                nc.vector.tensor_tensor(
-                    total[:, a:z], dx[b][:].indirect(pos2_t[:, a // 16 : z // 16]), first[:, a:z], ADD
-                )
+            for a, z in ((0, 640), (640, T)):
+                nc.gpsimd.tensor_tensor(total[:, a:z], first[:, a:z], second[:, a:z], ADD)
                 nc.sync.dma_start(out[b * P : (b + 1) * P, a:z], total[:, a:z])
 
-        for e in range(3):
-            quantize("early", [e], EARLY)
-            gather_words(e + 1, "raw_early_%d_1" % e)
-            for b in range(2):
-                multiply(e, b)
-        quantize("early", [3, 4], EARLY)
-        gather_words(4, "raw_early_4_1")
-        for e in (3, 4):
-            for b in range(2):
-                multiply(e, b)
+        quantize([0], 0, K)
+        gather_words(1)
+        for b in range(3):
+            multiply(0, b, b)
+        quantize([1], 0, K)
+        gather_words(2)
+        gate_staged("sumsA", [(0, 0), (0, 1)])
+        for b in range(3):
+            multiply(1, b, 3 + b)
+        quantize([2, 3], 0, P)
+        gather_words(3)
+        gate_staged("sumsB", [(1, 0)])
+        multiply(2, 0, 6)
+        multiply(3, 0, 7)
+        quantize([4], 0, P)
+        gather_words(4)
+        gate_staged("sumsC", [(1, 1), (2, 0)])
+        multiply(4, 0, 0)
+        gate_direct(4, 0)
+        quantize([2, 3], P, 2 * P, lambda: gate_staged("sumsD", [(3, 0)]))
+        first0 = fetch(0, pos1_t, "first0")
+        multiply(2, 1, 1)
+        multiply(3, 1, 3)
+        quantize([4], P, 2 * P)
+        second0 = fetch(0, pos2_t, "second0")
+        multiply(4, 1, 6)
+        gate_staged("sumsE", [(0, 2), (1, 2), (2, 1), (3, 1)])
+        gate_direct(4, 1)
+        add_and_store(0, first0, second0)
+        quantize([2, 3], 2 * P, K)
+        first1 = fetch(1, pos1_t, "first1")
+        multiply(2, 2, 7)
+        multiply(3, 2, 0)
+        quantize([4], 2 * P, K)
+        second1 = fetch(1, pos2_t, "second1")
+        multiply(4, 2, 1)
+        gate_staged("sumsF", [(2, 2), (3, 2)])
+        gate_direct(4, 2)
+        add_and_store(1, first1, second1)
 
-        halves = ((0, 640), (640, T))
-        first0 = fetch_first(0, halves, None)
-        fetch_second(0, first0, halves)
-        quantize("late", [0, 1, 2, 3], LATE)
-        quantize("late", [4], LATE)
-        first1 = fetch_first(1, halves, "raw_late_4_1")
-        fetch_second(1, first1, halves)
-        for e in range(E):
-            multiply(e, 2)
-        first2 = fetch_first(2, halves, None)
-        fetch_second(2, first2, ((0, 640), (640, 960), (960, T)))
+        first2 = sb([P, T], F32, "first2")
+        for a, z in ((0, 640), (640, T)):
+            nc.vector.tensor_copy(first2[:, a:z], dx[2][:].indirect(pos1_t[:, a // 16 : z // 16]))
+        total2 = sb([P, T], F32, "total2")
+        for a, z in ((0, 640), (640, 960), (960, T)):
+            nc.vector.tensor_tensor(total2[:, a:z], dx[2][:].indirect(pos2_t[:, a // 16 : z // 16]), first2[:, a:z], ADD)
+            nc.sync.dma_start(out[2 * P : 3 * P, a:z], total2[:, a:z])

from contextlib import ExitStack

import concourse.mybir as mybir

K, T, E, C, N = 384, 1280, 5, 512, 1024
S = E * C
FLOPS = 2 * N * K * S
BYTES = N * T + N // 32 * T + 4 * E * N * K + 4 * S + 2 * 128 * (S + 2 * T) // 16 + 4 * K * T

F32 = mybir.dt.float32
BF16 = mybir.dt.bfloat16
I32 = mybir.dt.int32
U32 = mybir.dt.uint32
U16 = mybir.dt.uint16
U8 = mybir.dt.uint8
E4X4 = mybir.dt.float8_e4m3fn_x4
E5X4 = mybir.dt.float8_e5m2_x4
MULT = mybir.AluOpType.mult
ADD = mybir.AluOpType.add

P = 128
PASSES = 2
ALIGN = 64
SCALE_WINDOW = 2048
SCALE_CUT = 2 * C
KB = 1024


def tile_moe_bdx_lin_none_kernel(tc, dy_words, dy_scales, w, gate, offs, pos1, pos2, out):
    nc = tc.nc
    with ExitStack() as ctx:
        keep = ctx.enter_context(tc.tile_pool(name="keep", bufs=1))
        arena = ctx.enter_context(tc.tile_pool(name="arena", bufs=1))
        psum = ctx.enter_context(tc.psum_pool(name="psum", bufs=1))

        at = {}
        at["word_win0"] = at["first2"] = 0
        at["word_win1"] = at["total2"] = 5 * KB
        at["raw_0_0_1"] = at["words1"] = 10 * KB
        at["raw_1_0_1"] = at["sumsA"] = 16 * KB
        at["words2"] = 21 * KB
        at["sumsB"] = 25 * KB
        at["raw_3_0_1"] = 26 * KB
        at["words3"] = 27 * KB
        at["sumsC"] = 31 * KB
        at["raw_4_0_1"] = 34 * KB
        at["words4"] = 35 * KB
        at["raw_2_128_1"] = at["sumsD"] = 39 * KB
        at["raw_3_128_1"] = at["first0"] = 41 * KB
        at["sumsE"] = at["total0"] = 46 * KB
        at["raw_4_128_1"] = 53 * KB
        at["second0"] = 54 * KB
        at["raw_3_256_1"] = at["first1"] = 59 * KB
        at["sumsF"] = at["total1"] = 64 * KB
        at["raw_4_256_1"] = 67 * KB + 512
        at["second1"] = 69 * KB

        def sb(shape, dtype, name):
            if name in at:
                return arena.tile(shape, dtype, name=name, align_bytes=ALIGN, offset=at[name])
            return keep.tile(shape, dtype, name=name, align_bytes=ALIGN)

        offs_t = keep.tile([P, S // 16], U16, name="offs_t")
        pos1_t = keep.tile([P, T // 16], U16, name="pos1_t")
        pos2_t = keep.tile([P, T // 16], U16, name="pos2_t")
        nc.sync.dma_start(offs_t[:], offs)

        scale_win = sb([P, SCALE_WINDOW], U8, "scale_win")
        nc.gpsimd.memset(scale_win[:].bitcast(I32), 0)
        for q in range(4):
            nc.scalar.dma_start(
                scale_win[32 * q : 32 * q + 8, 0:T].bitcast(I32),
                dy_scales[:, 4 * q : 4 * q + 4, :].bitcast(I32),
            )
        warm = sb([P, 16], F32, "warm")
        nc.gpsimd.memset(warm[:], 0.0)
        nc.scalar.copy(warm[:, 8:9], warm[:, 0:1])

        raw = {}

        def load_w(e, k0, k1, passes=(0, 1)):
            for o in passes:
                t = sb([P, 4, k1 - k0], F32, "raw_%d_%d_%d" % (e, k0, o))
                nc.sync.dma_start(
                    t[:], w[e, o * 512 : (o + 1) * 512, k0:k1].rearrange("(p j) k -> p j k", j=4)
                )
                raw[(e, k0, o)] = t

        word_win = []
        for o in range(PASSES):
            t = sb([P, T], U32, "word_win%d" % o)
            nc.sync.dma_start(t[:].bitcast(I32), dy_words[o].rearrange("p t d -> p (t d)").bitcast(I32))
            word_win.append(t)
            load_w(0, 0, K, (o,))

        cuts = ((0, SCALE_CUT), (SCALE_CUT, S))
        planes = {}

        def gather_scales(i, queue):
            a, b = cuts[i]
            both = sb([P, b - a], U8, "plane_both%d" % i)
            second = sb([P, b - a], U8, "plane_second%d" % i)
            nc.gpsimd.memset(second[:].bitcast(I32), 0)
            nc.vector.tensor_copy(both[:], scale_win[:].indirect(offs_t[:, a // 16 : b // 16]))
            queue.dma_start(second[0:112, :].bitcast(I32), both[4:116, :].bitcast(I32))
            planes[i] = (both, second)

        def dy_scale(e, o):
            i = 0 if e * C < SCALE_CUT else 1
            a = e * C - cuts[i][0]
            return planes[i][o][:, a : a + C]

        words = {}

        word_tiles = {}

        def gather_words(e, passes=(0, 1)):
            if e not in word_tiles:
                word_tiles[e] = sb([P, PASSES * C], U32, "words%d" % e)
            for o in passes:
                words[(e, o)] = word_tiles[e][:, o * C : (o + 1) * C]
                nc.vector.tensor_copy(
                    words[(e, o)], word_win[o][:].indirect(offs_t[:, e * C // 16 : (e + 1) * C // 16])
                )

        gather_scales(0, nc.scalar)
        gather_words(0, (0,))
        gather_scales(1, nc.gpsimd)
        gather_words(0, (1,))

        gate_t = sb([P, S], F32, "gate_t")
        load_w(1, 0, K)
        nc.sync.dma_start(gate_t[:, 0 : 2 * C], gate[0:P, 0 : 2 * C])
        for e in (2, 3, 4):
            load_w(e, 0, P)
        nc.sync.dma_start(gate_t[:, 2 * C : S], gate[0:P, 2 * C : S])
        nc.sync.dma_start(pos1_t[:], pos1)
        nc.sync.dma_start(pos2_t[:], pos2)
        for b in (1, 2):
            for e in (2, 3, 4):
                load_w(e, b * P, (b + 1) * P)

        codes = {}

        def quantize(experts, k0, k1, between=None):
            name = "%d_%d" % (experts[0], k0)
            width = k1 - k0
            cols = len(experts) * PASSES * width
            grouped = sb([P, cols * 4], BF16, "grouped_" + name)
            cw = sb([P, cols], U32, "codes_" + name)
            cs = sb([P, cols], U8, "scales_" + name)
            for n, e in enumerate(experts):
                for o in range(PASSES):
                    c0 = (n * PASSES + o) * width
                    nc.scalar.copy(
                        grouped[:, 4 * c0 : 4 * (c0 + width)].rearrange("p (c i t) -> p c t i", i=4, t=4),
                        raw[(e, k0, o)][:].rearrange("p t (c i) -> p c t i", i=4),
                    )
                    for k in range(k0, k1, P):
                        c = c0 + k - k0
                        codes[(e, k // P, o)] = (cw[:, c : c + P], cs[:, c : c + P])
                if between and n == 0:
                    between()
            for a, z in ((0, 512), (512, 768)) if cols == 768 else ((0, cols),):
                nc.vector.quantize_mx(out=cw[:, a:z].bitcast(E4X4), scales=cs[:, a:z], in_=grouped[:, 4 * a : 4 * z])

        dx = [sb([P, S], F32, "dx%d" % b) for b in range(K // P)]
        acc = {}

        def multiply(e, b, bank):
            acc[(e, b)] = psum.tile([P, C], F32, name="acc%d_%d" % (e, b), tag="bank%d" % bank)
            for o in range(PASSES):
                cw, cs = codes[(e, b, o)]
                nc.tensor.matmul_mx(
                    out=acc[(e, b)][:],
                    lhsT=cw.bitcast(E4X4),
                    lhsT_scale=cs,
                    rhs=words[(e, o)].bitcast(E5X4),
                    rhs_scale=dy_scale(e, o),
                    start=(o == 0),
                    stop=(o == PASSES - 1),
                )

        def gate_direct(e, b):
            cols = slice(e * C, (e + 1) * C)
            nc.vector.tensor_tensor(dx[b][:, cols], acc[(e, b)][:], gate_t[:, cols], MULT)

        def gate_staged(name, units):
            sums = sb([P, len(units) * C], F32, name)
            for n, (e, b) in enumerate(units):
                cols = slice(e * C, (e + 1) * C)
                nc.scalar.copy(sums[:, n * C : (n + 1) * C], acc[(e, b)][:])
                nc.gpsimd.tensor_tensor(dx[b][:, cols], sums[:, n * C : (n + 1) * C], gate_t[:, cols], MULT)

        def fetch(b, pos_t, name):
            t = sb([P, T], F32, name)
            nc.vector.tensor_copy(t[:], dx[b][:].indirect(pos_t[:]))
            return t

        def add_and_store(b, first, second):
            total = sb([P, T], F32, "total%d" % b)
            for a, z in ((0, 640), (640, T)):
                nc.gpsimd.tensor_tensor(total[:, a:z], first[:, a:z], second[:, a:z], ADD)
                nc.sync.dma_start(out[b * P : (b + 1) * P, a:z], total[:, a:z])

        quantize([0], 0, K)
        gather_words(1)
        for b in range(3):
            multiply(0, b, b)
        quantize([1], 0, K)
        gather_words(2)
        gate_staged("sumsA", [(0, 0), (0, 1)])
        for b in range(3):
            multiply(1, b, 3 + b)
        quantize([2, 3], 0, P)
        gather_words(3)
        gate_staged("sumsB", [(1, 0)])
        multiply(2, 0, 6)
        multiply(3, 0, 7)
        quantize([4], 0, P)
        gather_words(4)
        gate_staged("sumsC", [(1, 1), (2, 0)])
        multiply(4, 0, 0)
        gate_direct(4, 0)
        quantize([2, 3], P, 2 * P, lambda: gate_staged("sumsD", [(3, 0)]))
        first0 = fetch(0, pos1_t, "first0")
        multiply(2, 1, 1)
        multiply(3, 1, 3)
        quantize([4], P, 2 * P)
        second0 = fetch(0, pos2_t, "second0")
        multiply(4, 1, 6)
        gate_staged("sumsE", [(0, 2), (1, 2), (2, 1), (3, 1)])
        gate_direct(4, 1)
        add_and_store(0, first0, second0)
        quantize([2, 3], 2 * P, K)
        first1 = fetch(1, pos1_t, "first1")
        multiply(2, 2, 7)
        multiply(3, 2, 0)
        quantize([4], 2 * P, K)
        second1 = fetch(1, pos2_t, "second1")
        multiply(4, 2, 1)
        gate_staged("sumsF", [(2, 2), (3, 2)])
        gate_direct(4, 2)
        add_and_store(1, first1, second1)

        first2 = sb([P, T], F32, "first2")
        for a, z in ((0, 640), (640, T)):
            nc.vector.tensor_copy(first2[:, a:z], dx[2][:].indirect(pos1_t[:, a // 16 : z // 16]))
        total2 = sb([P, T], F32, "total2")
        for a, z in ((0, 640), (640, 960), (960, T)):
            nc.vector.tensor_tensor(total2[:, a:z], dx[2][:].indirect(pos2_t[:, a // 16 : z // 16]), first2[:, a:z], ADD)
            nc.sync.dma_start(out[2 * P : 3 * P, a:z], total2[:, a:z])
